import numpy as np
import ml_dtypes


def mxq(x, axis, fmt="e4m3"):
    dtype, down = {"e4m3": (ml_dtypes.float8_e4m3fn, 7), "e5m2": (ml_dtypes.float8_e5m2, 14)}[fmt]
    v = np.moveaxis(np.asarray(x, np.float32).astype(ml_dtypes.bfloat16).astype(np.float64), axis, -1)
    blocks = v.reshape(v.shape[:-1] + (-1, 32))
    amax = np.abs(blocks).max(-1, keepdims=True)
    byte = np.maximum(np.where(amax > 0, np.frexp(amax)[1] - 1 + 127, 0) - down, 1)
    scale = np.exp2(byte - 127.0)
    codes = (blocks / scale).astype(np.float32).astype(dtype).astype(np.float64)
    return np.moveaxis((codes * scale).reshape(v.shape), -1, axis)


WIDE = False


def mx_kscale(k):
    if not WIDE:
        return np.ones(k)
    levels = np.array([10, -10, 5, -5, 0])
    if k % 512:
        return np.exp2(np.random.permutation(np.resize(levels, k // 32))).repeat(32)
    a = np.empty((k // 512, 16))
    for p in range(k // 512):
        a[p, :8] = np.random.permutation(np.resize(levels, 8))
        for g in range(8):
            far = levels[np.abs(levels - a[p, g]) >= 10]
            a[p, g + 8] = far[np.random.randint(len(far))]
    return np.exp2(a.ravel()).repeat(32)


def f64(x):
    return np.asarray(x).astype(np.float64)


def striped8(idx):
    return np.concatenate([x.reshape(-1, 16).T for x in idx]).astype(np.uint16)


def runs(offs, k):
    lists = np.stack([offs[16 * r : 16 * r + 16].T.reshape(-1) for r in range(8)]).astype(np.int64)
    return lists[np.arange(k) % 512 // 64]


def pack_weight(w):
    k, n = w.shape
    w = f64(np.asarray(w, np.float32).astype(ml_dtypes.bfloat16)).reshape(k // 32, 32, n)
    amax = np.abs(w).max(1)
    byte = np.clip(np.where(amax > 0, np.frexp(amax)[1] - 1 + 127 - 7, 1), 1, 254)
    scaled = (w * np.exp2(127.0 - byte)[:, None, :]).reshape(k, n).astype(np.float32)
    words = np.ascontiguousarray(scaled.reshape(k // 512, 128, 4, n).transpose(0, 1, 3, 2)).astype(ml_dtypes.float8_e4m3fn).view(np.uint8)
    return words, np.ascontiguousarray(byte.astype(np.uint8).reshape(k // 512, 16, n))


def unpack_weight(words, scales):
    g, p, n, _ = words.shape
    vals = np.ascontiguousarray(words).view(ml_dtypes.float8_e4m3fn).astype(np.float64) * np.repeat(np.exp2(scales.astype(np.float64) - 127.0), 8, axis=1)[..., None]
    return vals.transpose(0, 1, 3, 2).reshape(g * 512, n)


K, T, S, N, H = 512, 2048, 512, 512, 512


def setup_inputs():
    n = np.random.standard_normal
    s = mx_kscale(K)[:, None]
    u = mx_kscale(H)
    packed_xT = pack_weight(n((K, T)) * s)
    return {
        "x_words": packed_xT[0],
        "x_scales": packed_xT[1],
        "w1": (n((K, H)) / np.sqrt(K) / s).astype(np.float32),
        "gn": (np.random.uniform(0.5, 1.5, (H, 1)) * u[:, None]).astype(np.float32),
        "w2": (n((H, N)) / np.sqrt(H) / u[:, None]).astype(np.float32),
        "offs": striped8(np.random.randint(0, T, (8, S))),
        "n1": striped8(np.stack([np.random.permutation(S) for _ in range(8)])),
        "n2": striped8(np.stack([np.random.permutation(S) for _ in range(8)])),
        "n3": striped8(np.stack([np.random.permutation(S) for _ in range(8)])),
        "n4": striped8(np.stack([np.random.permutation(S) for _ in range(8)])),
        "n5": striped8(np.stack([np.random.permutation(S) for _ in range(8)])),
    }


def reference(x_words, x_scales, w1, gn, w2, offs, n1, n2, n3, n4, n5):
    xq = unpack_weight(x_words, x_scales)[np.arange(K)[:, None], runs(offs, K)]
    y = mxq(f64(w1), 0, "e4m3").T @ xq
    ex = np.exp(0.5 * y)
    z = f64(gn) * (np.log((ex + ex[np.arange(H)[:, None], runs(n1, H)]) / (ex[np.arange(H)[:, None], runs(n2, H)] + ex[np.arange(H)[:, None], runs(n3, H)])))
    h = mxq(f64(w2), 0, "e4m3").T @ mxq(z, 0, "e4m3")
    return (h[np.arange(N)[:, None], runs(n4, N)]) * (h[np.arange(N)[:, None], runs(n5, N)])

@@ -1,0 +1,192 @@
+from contextlib import ExitStack
+
+import concourse.mybir as mybir
+
+K, T, S, N, H = 512, 2048, 512, 512, 512
+FLOPS = 2 * K * H * S + 2 * H * N * S
+
+F32 = mybir.dt.float32
+BF16 = mybir.dt.bfloat16
+I32 = mybir.dt.int32
+U32 = mybir.dt.uint32
+U16 = mybir.dt.uint16
+U8 = mybir.dt.uint8
+FP8X4 = mybir.dt.float8_e4m3fn_x4
+ALU = mybir.AluOpType
+ACT = mybir.ActivationFunctionType
+
+P = 128
+PACK = 4
+HALF = S // 2
+LCOLS = HALF // 16
+ACT_TILES = (1, 2, 3)
+
+
+def tile_picked_hashoddsprod_none_p_kernel(tc, x_words, x_scales, w1, gn, w2, offs, n1, n2, n3, n4, n5, out):
+    nc = tc.nc
+    with ExitStack() as ctx:
+        keep = ctx.enter_context(tc.tile_pool(name="keep", bufs=1))
+        psum = ctx.enter_context(tc.psum_pool(name="psum", bufs=1))
+
+        def load_list(src, name):
+            tile = keep.tile([P, S // 16], U16, name=name)
+            nc.sync.dma_start(tile[:], src)
+            return tile
+
+        def half_of(tile, h):
+            return tile[:, h * LCOLS : (h + 1) * LCOLS]
+
+        def cols(h):
+            return slice(h * HALF, (h + 1) * HALF)
+
+        scale_win = keep.tile([P, T], U8, name="scale_win")
+        nc.vector.memset(scale_win[:].bitcast(I32), 0)
+        x_plane = keep.tile([P, S], U8, name="x_plane", align_bytes=64)
+        nc.vector.memset(x_plane[:].bitcast(I32), 0)
+
+        offs_t = load_list(offs, "offs_t")
+        for q in range(4):
+            nc.scalar.dma_start(
+                scale_win[32 * q + 14 : 32 * q + 18, :].bitcast(I32),
+                x_scales[0, 4 * q : 4 * q + 4, :].bitcast(I32),
+            )
+        word_win = keep.tile([P, T], U32, name="word_win")
+        nc.sync.dma_start(
+            word_win[:].bitcast(I32), x_words[0].rearrange("p n r -> p (n r)").bitcast(I32)
+        )
+
+        def load_w(w, name):
+            halves = []
+            for c in range(2):
+                raw = keep.tile([P, PACK, 256], F32, name=f"{name}_raw{c}")
+                nc.sync.dma_start(
+                    raw[:], w.rearrange("(p j) c -> p j c", j=PACK)[:, :, 256 * c : 256 * (c + 1)]
+                )
+                halves.append(raw)
+            return halves
+
+        w1_raw = load_w(w1, "w1")
+        n1_t = load_list(n1, "n1_t")
+        n2_t = load_list(n2, "n2_t")
+        n3_t = load_list(n3, "n3_t")
+        gain = keep.tile([P, PACK], F32, name="gain")
+        nc.sync.dma_start(gain[:], gn.rearrange("(p t) o -> p (t o)", t=PACK))
+        w2_raw = load_w(w2, "w2")
+        n4_t = load_list(n4, "n4_t")
+        n5_t = load_list(n5, "n5_t")
+
+        scale_got = keep.tile([P, S], U8, name="scale_got")
+        nc.vector.tensor_copy(scale_got[:], scale_win[:].indirect(offs_t[:]))
+        nc.scalar.dma_start(x_plane[0:114, :].bitcast(I32), scale_got[14:128, :].bitcast(I32))
+        x_codes = keep.tile([P, S], U32, name="x_codes", align_bytes=64)
+        nc.vector.tensor_copy(x_codes[:], word_win[:].indirect(offs_t[:]))
+
+        def deal(raw, grouped, c, copy):
+            dst = grouped[:].rearrange("p (t m j) -> p m j t", t=PACK, j=PACK)[:, 64 * c : 64 * (c + 1), :, :]
+            copy(dst, raw[:].rearrange("p j (m t) -> p m j t", t=PACK))
+
+        def quantize_w(grouped, name):
+            codes = keep.tile([P, 512], U32, name=f"{name}_codes", align_bytes=64)
+            scales = keep.tile([P, 512], U8, name=f"{name}_scales", align_bytes=64)
+            return codes, scales
+
+        w1_bf = keep.tile([P, 2048], BF16, name="w1_bf", align_bytes=64)
+        deal(w1_raw[0], w1_bf, 0, nc.scalar.copy)
+        deal(w1_raw[1], w1_bf, 1, nc.vector.tensor_copy)
+        w1_codes, w1_scales = quantize_w(w1_bf, "w1")
+
+        y_ps = []
+        for t in range(PACK):
+            m = slice(P * t, P * (t + 1))
+            nc.vector.quantize_mx(
+                w1_codes[:, m].bitcast(FP8X4), w1_scales[:, m], w1_bf[:, 512 * t : 512 * (t + 1)]
+            )
+            y = psum.tile([P, S], F32, name=f"y{t}")
+            nc.tensor.matmul_mx(
+                y[:], lhsT=w1_codes[:, m].bitcast(FP8X4), lhsT_scale=w1_scales[:, m],
+                rhs=x_codes[:].bitcast(FP8X4), rhs_scale=x_plane[:], start=True, stop=True,
+            )
+            y_ps.append(y)
+
+        ex = []
+        for t in range(PACK):
+            e = keep.tile([P, S], F32, name=f"ex{t}")
+            nc.scalar.activation(e[:], y_ps[t][:], ACT.Exp, scale=0.5)
+            ex.append(e)
+        half_y = {}
+        for t in ACT_TILES:
+            a = keep.tile([P, S], F32, name=f"half_y{t}")
+            nc.vector.tensor_scalar(a[:], y_ps[t][:], 0.5, None, ALU.mult)
+            half_y[t] = a
+
+        num = [keep.tile([P, PACK, HALF], F32, name=f"num{h}") for h in range(2)]
+        den = [keep.tile([P, PACK, HALF], F32, name=f"den{h}") for h in range(2)]
+        g1 = {}
+        g2 = {}
+        for h in range(2):
+            for t in range(PACK):
+                g1[h, t] = keep.tile([P, HALF], F32, name=f"g1_{h}{t}")
+                g2[h, t] = keep.tile([P, HALF], F32, name=f"g2_{h}{t}")
+        for h in range(2):
+            for t in ACT_TILES:
+                nc.scalar.activation(g2[h, t][:], half_y[t][:].indirect(half_of(n2_t, h)), ACT.Exp)
+                nc.scalar.activation(g1[h, t][:], half_y[t][:].indirect(half_of(n1_t, h)), ACT.Exp)
+        for h in range(2):
+            nc.vector.tensor_copy(g2[h, 0][:], ex[0][:].indirect(half_of(n2_t, h)))
+            nc.vector.tensor_copy(g1[h, 0][:], ex[0][:].indirect(half_of(n1_t, h)))
+
+        w2_bf = keep.tile([P, 2048], BF16, name="w2_bf", align_bytes=64)
+        deal(w2_raw[0], w2_bf, 0, nc.vector.tensor_copy)
+        deal(w2_raw[1], w2_bf, 1, nc.vector.tensor_copy)
+        w2_codes, w2_scales = quantize_w(w2_bf, "w2")
+
+        for h in range(2):
+            for t in range(PACK):
+                nc.vector.tensor_tensor(
+                    den[h][:, t, :], ex[t][:].indirect(half_of(n3_t, h)), g2[h, t][:], ALU.add
+                )
+                nc.vector.tensor_tensor(num[h][:, t, :], g1[h, t][:], ex[t][:, cols(h)], ALU.add)
+            if h == 0:
+                nc.vector.quantize_mx(w2_codes[:].bitcast(FP8X4), w2_scales[:], w2_bf[:])
+
+        z_codes = keep.tile([P, S], U32, name="z_codes", align_bytes=64)
+        z_scales = keep.tile([P, S], U8, name="z_scales", align_bytes=64)
+        h_ps = [psum.tile([P, S], F32, name=f"h{t}") for t in range(PACK)]
+        Q = 128
+        for c in range(S // Q):
+            h, part = divmod(c, 2)
+            pc = slice(Q * part, Q * (part + 1))
+            ln_num = keep.tile([P, PACK, Q], F32, name=f"ln_num{c}")
+            ln_den = keep.tile([P, PACK, Q], F32, name=f"ln_den{c}")
+            nc.scalar.activation(ln_num[:], num[h][:, :, pc], ACT.Ln)
+            nc.scalar.activation(ln_den[:], den[h][:, :, pc], ACT.Ln)
+            odds = keep.tile([P, PACK, Q], F32, name=f"odds{c}")
+            nc.vector.tensor_tensor(odds[:], ln_num[:], ln_den[:], ALU.subtract)
+            z_bf = keep.tile([P, Q, PACK], BF16, name=f"z_bf{c}", align_bytes=64)
+            nc.vector.tensor_tensor(
+                z_bf[:].rearrange("p (c i) t -> p c t i", i=4),
+                odds[:].rearrange("p t (c i) -> p c t i", i=4),
+                gain[:].unsqueeze(1).unsqueeze(3).to_broadcast([P, Q // 4, PACK, 4]),
+                ALU.mult,
+            )
+            zc = slice(Q * c, Q * (c + 1))
+            nc.vector.quantize_mx(
+                z_codes[:, zc].bitcast(FP8X4), z_scales[:, zc], z_bf[:].rearrange("p c t -> p (c t)")
+            )
+            for t in range(PACK):
+                m = slice(P * t, P * (t + 1))
+                nc.tensor.matmul_mx(
+                    h_ps[t][:, zc], lhsT=w2_codes[:, m].bitcast(FP8X4), lhsT_scale=w2_scales[:, m],
+                    rhs=z_codes[:, zc].bitcast(FP8X4), rhs_scale=z_scales[:, zc], start=True, stop=True,
+                )
+
+        out_rows = out.rearrange("(p t) j -> p t j", t=PACK)
+        for t in range(PACK):
+            hs = keep.tile([P, S], F32, name=f"hs{t}")
+            nc.scalar.copy(hs[:], h_ps[t][:])
+            res = keep.tile([P, S], F32, name=f"res{t}")
+            for h in range(2):
+                g4 = keep.tile([P, HALF], F32, name=f"g4_{t}{h}")
+                nc.vector.tensor_copy(g4[:], hs[:].indirect(half_of(n4_t, h)))
+                nc.vector.tensor_tensor(res[:, cols(h)], hs[:].indirect(half_of(n5_t, h)), g4[:], ALU.mult)
+            nc.sync.dma_start(out_rows[:, t, :], res[:])

@@ -19,7 +19,7 @@ P = 128
 PACK = 4
 HALF = S // 2
 LCOLS = HALF // 16
-ACT_TILES = (1, 2, 3)
+Q = 128
 
 
 def tile_picked_hashoddsprod_none_p_kernel(tc, x_words, x_scales, w1, gn, w2, offs, n1, n2, n3, n4, n5, out):
@@ -39,53 +39,53 @@ def tile_picked_hashoddsprod_none_p_kernel(tc, x_words, x_scales, w1, gn, w2, of
         def cols(h):
             return slice(h * HALF, (h + 1) * HALF)
 
-        scale_win = keep.tile([P, T], U8, name="scale_win")
-        nc.vector.memset(scale_win[:].bitcast(I32), 0)
-        x_plane = keep.tile([P, S], U8, name="x_plane", align_bytes=64)
-        nc.vector.memset(x_plane[:].bitcast(I32), 0)
-
         offs_t = load_list(offs, "offs_t")
-        for q in range(4):
-            nc.scalar.dma_start(
-                scale_win[32 * q + 14 : 32 * q + 18, :].bitcast(I32),
-                x_scales[0, 4 * q : 4 * q + 4, :].bitcast(I32),
+        scale_win = keep.tile([P, T], U8, name="scale_win", tag="slot_a")
+        scale_rows = x_scales[0].bitcast(I32).rearrange("(g e) c -> e g c", e=2)
+        for e in range(2):
+            nc.sync.dma_start(
+                scale_win[e:P:2, :].bitcast(I32),
+                scale_rows[e].unsqueeze(1).to_broadcast([8, 8, T // 4]),
             )
-        word_win = keep.tile([P, T], U32, name="word_win")
+        word_win = keep.tile([P, T], U32, name="word_win", tag="slot_b")
         nc.sync.dma_start(
             word_win[:].bitcast(I32), x_words[0].rearrange("p n r -> p (n r)").bitcast(I32)
         )
 
-        def load_w(w, name):
+        def load_w(w, name, tags):
             halves = []
             for c in range(2):
-                raw = keep.tile([P, PACK, 256], F32, name=f"{name}_raw{c}")
+                raw = keep.tile([P, PACK, 256], F32, name=f"{name}_raw{c}", tag=tags[c])
                 nc.sync.dma_start(
                     raw[:], w.rearrange("(p j) c -> p j c", j=PACK)[:, :, 256 * c : 256 * (c + 1)]
                 )
                 halves.append(raw)
             return halves
 
-        w1_raw = load_w(w1, "w1")
-        n1_t = load_list(n1, "n1_t")
+        w1_raw = load_w(w1, "w1", ("w1a", "w1b"))
         n2_t = load_list(n2, "n2_t")
         n3_t = load_list(n3, "n3_t")
+        n1_t = load_list(n1, "n1_t")
         gain = keep.tile([P, PACK], F32, name="gain")
         nc.sync.dma_start(gain[:], gn.rearrange("(p t) o -> p (t o)", t=PACK))
-        w2_raw = load_w(w2, "w2")
         n4_t = load_list(n4, "n4_t")
         n5_t = load_list(n5, "n5_t")
 
+        x_plane = keep.tile([P, S], U8, name="x_plane", align_bytes=64)
+        nc.vector.memset(x_plane[:].bitcast(I32), 0)
         scale_got = keep.tile([P, S], U8, name="scale_got")
         nc.vector.tensor_copy(scale_got[:], scale_win[:].indirect(offs_t[:]))
-        nc.scalar.dma_start(x_plane[0:114, :].bitcast(I32), scale_got[14:128, :].bitcast(I32))
+        nc.scalar.dma_start(x_plane[0:112, :].bitcast(I32), scale_got[14:126, :].bitcast(I32))
         x_codes = keep.tile([P, S], U32, name="x_codes", align_bytes=64)
         nc.vector.tensor_copy(x_codes[:], word_win[:].indirect(offs_t[:]))
+
+        w2_raw = load_w(w2, "w2", ("slot_a", "slot_b"))
 
         def deal(raw, grouped, c, copy):
             dst = grouped[:].rearrange("p (t m j) -> p m j t", t=PACK, j=PACK)[:, 64 * c : 64 * (c + 1), :, :]
             copy(dst, raw[:].rearrange("p j (m t) -> p m j t", t=PACK))
 
-        def quantize_w(grouped, name):
+        def mx_tiles(name):
             codes = keep.tile([P, 512], U32, name=f"{name}_codes", align_bytes=64)
             scales = keep.tile([P, 512], U8, name=f"{name}_scales", align_bytes=64)
             return codes, scales
@@ -93,7 +93,7 @@ def tile_picked_hashoddsprod_none_p_kernel(tc, x_words, x_scales, w1, gn, w2, of
         w1_bf = keep.tile([P, 2048], BF16, name="w1_bf", align_bytes=64)
         deal(w1_raw[0], w1_bf, 0, nc.scalar.copy)
         deal(w1_raw[1], w1_bf, 1, nc.vector.tensor_copy)
-        w1_codes, w1_scales = quantize_w(w1_bf, "w1")
+        w1_codes, w1_scales = mx_tiles("w1")
 
         y_ps = []
         for t in range(PACK):
@@ -108,85 +108,127 @@ def tile_picked_hashoddsprod_none_p_kernel(tc, x_words, x_scales, w1, gn, w2, of
             )
             y_ps.append(y)
 
-        ex = []
+        N2_ON_ACT = (1, 2, 3)
+        N1_ON_ACT = (2, 3)
+        ex, twin, half_y = {}, {}, {}
         for t in range(PACK):
-            e = keep.tile([P, S], F32, name=f"ex{t}")
-            nc.scalar.activation(e[:], y_ps[t][:], ACT.Exp, scale=0.5)
-            ex.append(e)
-        half_y = {}
-        for t in ACT_TILES:
-            a = keep.tile([P, S], F32, name=f"half_y{t}")
-            nc.vector.tensor_scalar(a[:], y_ps[t][:], 0.5, None, ALU.mult)
-            half_y[t] = a
+            ex[t] = keep.tile([P, S], F32, name=f"ex{t}")
+            nc.scalar.activation(ex[t][:], y_ps[t][:], ACT.Exp, scale=0.5)
+            if t not in N1_ON_ACT:
+                twin[t] = keep.tile([P, S], F32, name=f"twin{t}")
+                nc.sync.dma_start(twin[t][:], ex[t][:])
+            if t in N2_ON_ACT:
+                half_y[t] = keep.tile([P, S], F32, name=f"half_y{t}")
+                nc.scalar.activation(half_y[t][:], y_ps[t][:], ACT.Copy, scale=0.5)
 
         num = [keep.tile([P, PACK, HALF], F32, name=f"num{h}") for h in range(2)]
         den = [keep.tile([P, PACK, HALF], F32, name=f"den{h}") for h in range(2)]
-        g1 = {}
-        g2 = {}
+        g1, g2 = {}, {}
         for h in range(2):
-            for t in range(PACK):
-                g1[h, t] = keep.tile([P, HALF], F32, name=f"g1_{h}{t}")
+            for t in N2_ON_ACT:
                 g2[h, t] = keep.tile([P, HALF], F32, name=f"g2_{h}{t}")
-        for h in range(2):
-            for t in ACT_TILES:
                 nc.scalar.activation(g2[h, t][:], half_y[t][:].indirect(half_of(n2_t, h)), ACT.Exp)
-                nc.scalar.activation(g1[h, t][:], half_y[t][:].indirect(half_of(n1_t, h)), ACT.Exp)
-        for h in range(2):
-            nc.vector.tensor_copy(g2[h, 0][:], ex[0][:].indirect(half_of(n2_t, h)))
-            nc.vector.tensor_copy(g1[h, 0][:], ex[0][:].indirect(half_of(n1_t, h)))
+                if t in N1_ON_ACT:
+                    g1[h, t] = keep.tile([P, HALF], F32, name=f"g1_{h}{t}")
+                    nc.scalar.activation(g1[h, t][:], half_y[t][:].indirect(half_of(n1_t, h)), ACT.Exp)
+
+        def make_den(h, t):
+            nc.vector.tensor_tensor(den[h][:, t, :], ex[t][:].indirect(half_of(n3_t, h)), g2[h, t][:], ALU.add)
+
+        def make_num(h, t):
+            if t in N1_ON_ACT:
+                nc.vector.tensor_tensor(num[h][:, t, :], g1[h, t][:], ex[t][:, cols(h)], ALU.add)
+            else:
+                nc.vector.tensor_tensor(
+                    num[h][:, t, :], ex[t][:].indirect(half_of(n1_t, h)), twin[t][:, cols(h)], ALU.add
+                )
 
         w2_bf = keep.tile([P, 2048], BF16, name="w2_bf", align_bytes=64)
+        w2_codes, w2_scales = mx_tiles("w2")
         deal(w2_raw[0], w2_bf, 0, nc.vector.tensor_copy)
-        deal(w2_raw[1], w2_bf, 1, nc.vector.tensor_copy)
-        w2_codes, w2_scales = quantize_w(w2_bf, "w2")
-
         for h in range(2):
-            for t in range(PACK):
-                nc.vector.tensor_tensor(
-                    den[h][:, t, :], ex[t][:].indirect(half_of(n3_t, h)), g2[h, t][:], ALU.add
-                )
-                nc.vector.tensor_tensor(num[h][:, t, :], g1[h, t][:], ex[t][:, cols(h)], ALU.add)
-            if h == 0:
-                nc.vector.quantize_mx(w2_codes[:].bitcast(FP8X4), w2_scales[:], w2_bf[:])
+            g2[h, 0] = keep.tile([P, HALF], F32, name=f"g2_{h}0")
+            nc.vector.tensor_copy(g2[h, 0][:], ex[0][:].indirect(half_of(n2_t, h)))
+        deal(w2_raw[1], w2_bf, 1, nc.vector.tensor_copy)
+        for h in range(2):
+            make_den(h, 0)
+        nc.vector.quantize_mx(w2_codes[:].bitcast(FP8X4), w2_scales[:], w2_bf[:])
+        for h in range(2):
+            make_num(h, 0)
+            for t in range(1, PACK):
+                make_den(h, t)
+                make_num(h, t)
 
-        z_codes = keep.tile([P, S], U32, name="z_codes", align_bytes=64)
-        z_scales = keep.tile([P, S], U8, name="z_scales", align_bytes=64)
+        z_codes, z_scales = mx_tiles("z")
         h_ps = [psum.tile([P, S], F32, name=f"h{t}") for t in range(PACK)]
-        Q = 128
-        for c in range(S // Q):
+        hs = [keep.tile([P, S], F32, name=f"hs{t}") for t in range(PACK)]
+        chunks = S // Q
+        last = chunks - 1
+        ln_num, ln_den, odds, z_bf = {}, {}, {}, {}
+
+        def logs(c):
             h, part = divmod(c, 2)
             pc = slice(Q * part, Q * (part + 1))
-            ln_num = keep.tile([P, PACK, Q], F32, name=f"ln_num{c}")
-            ln_den = keep.tile([P, PACK, Q], F32, name=f"ln_den{c}")
-            nc.scalar.activation(ln_num[:], num[h][:, :, pc], ACT.Ln)
-            nc.scalar.activation(ln_den[:], den[h][:, :, pc], ACT.Ln)
-            odds = keep.tile([P, PACK, Q], F32, name=f"odds{c}")
-            nc.vector.tensor_tensor(odds[:], ln_num[:], ln_den[:], ALU.subtract)
-            z_bf = keep.tile([P, Q, PACK], BF16, name=f"z_bf{c}", align_bytes=64)
+            ln_num[c] = keep.tile([P, PACK, Q], F32, name=f"ln_num{c}")
+            ln_den[c] = keep.tile([P, PACK, Q], F32, name=f"ln_den{c}")
+            nc.scalar.activation(ln_den[c][:], den[h][:, :, pc], ACT.Ln)
+            nc.scalar.activation(ln_num[c][:], num[h][:, :, pc], ACT.Ln)
+
+        def subtract(c):
+            odds[c] = keep.tile([P, PACK, Q], F32, name=f"odds{c}")
+            nc.vector.tensor_tensor(odds[c][:], ln_num[c][:], ln_den[c][:], ALU.subtract)
+
+        def scale(c):
+            z_bf[c] = keep.tile([P, Q, PACK], BF16, name=f"z_bf{c}", align_bytes=64)
             nc.vector.tensor_tensor(
-                z_bf[:].rearrange("p (c i) t -> p c t i", i=4),
-                odds[:].rearrange("p t (c i) -> p c t i", i=4),
+                z_bf[c][:].rearrange("p (c i) t -> p c t i", i=4),
+                odds[c][:].rearrange("p t (c i) -> p c t i", i=4),
                 gain[:].unsqueeze(1).unsqueeze(3).to_broadcast([P, Q // 4, PACK, 4]),
                 ALU.mult,
             )
+
+        def project(c):
             zc = slice(Q * c, Q * (c + 1))
             nc.vector.quantize_mx(
-                z_codes[:, zc].bitcast(FP8X4), z_scales[:, zc], z_bf[:].rearrange("p c t -> p (c t)")
+                z_codes[:, zc].bitcast(FP8X4), z_scales[:, zc], z_bf[c][:].rearrange("p c t -> p (c t)")
             )
             for t in range(PACK):
                 m = slice(P * t, P * (t + 1))
+                if t == 0 and c == last:
+                    h0_end = psum.tile([P, Q], F32, name="y0")
+                    dst = h0_end[:]
+                else:
+                    dst = h_ps[t][:, zc]
                 nc.tensor.matmul_mx(
-                    h_ps[t][:, zc], lhsT=w2_codes[:, m].bitcast(FP8X4), lhsT_scale=w2_scales[:, m],
+                    dst, lhsT=w2_codes[:, m].bitcast(FP8X4), lhsT_scale=w2_scales[:, m],
                     rhs=z_codes[:, zc].bitcast(FP8X4), rhs_scale=z_scales[:, zc], start=True, stop=True,
                 )
+                if t == 0 and c == last - 1:
+                    nc.scalar.copy(hs[0][:, : Q * last], h_ps[0][:, : Q * last])
+                if t == 0 and c == last:
+                    nc.scalar.copy(hs[0][:, zc], dst)
+
+        for c in range(chunks):
+            logs(c)
+        for step in range(chunks + 2):
+            if step < chunks:
+                subtract(step)
+            if 2 <= step:
+                project(step - 2)
+            if 1 <= step <= chunks:
+                scale(step - 1)
 
         out_rows = out.rearrange("(p t) j -> p t j", t=PACK)
         for t in range(PACK):
-            hs = keep.tile([P, S], F32, name=f"hs{t}")
-            nc.scalar.copy(hs[:], h_ps[t][:])
+            if t > 0:
+                nc.scalar.copy(hs[t][:], h_ps[t][:])
+            g4 = keep.tile([P, S], F32, name=f"g4_{t}")
+            for h in range(2):
+                nc.vector.tensor_copy(g4[:, cols(h)], hs[t][:].indirect(half_of(n4_t, h)))
             res = keep.tile([P, S], F32, name=f"res{t}")
             for h in range(2):
-                g4 = keep.tile([P, HALF], F32, name=f"g4_{t}{h}")
-                nc.vector.tensor_copy(g4[:], hs[:].indirect(half_of(n4_t, h)))
-                nc.vector.tensor_tensor(res[:, cols(h)], hs[:].indirect(half_of(n5_t, h)), g4[:], ALU.mult)
-            nc.sync.dma_start(out_rows[:, t, :], res[:])
+                nc.vector.tensor_tensor(res[:, cols(h)], hs[t][:].indirect(half_of(n5_t, h)), g4[:, cols(h)], ALU.mult)
+                if t == PACK - 1:
+                    nc.sync.dma_start(out_rows[:, t, cols(h)], res[:, cols(h)])
+            if t < PACK - 1:
+                nc.sync.dma_start(out_rows[:, t, :], res[:])

@@ -39,6 +39,9 @@ def tile_picked_hashoddsprod_none_p_kernel(tc, x_words, x_scales, w1, gn, w2, of
         def cols(h):
             return slice(h * HALF, (h + 1) * HALF)
 
+        warm = keep.tile([P, 2], F32, name="warm")
+        nc.vector.memset(warm[:, 0:1], 0.0)
+        nc.scalar.activation(warm[:, 1:2], warm[:, 0:1], ACT.Exp)
         offs_t = load_list(offs, "offs_t")
         scale_win = keep.tile([P, T], U8, name="scale_win", tag="slot_a")
         scale_rows = x_scales[0].bitcast(I32).rearrange("(g e) c -> e g c", e=2)
@@ -47,7 +50,11 @@ def tile_picked_hashoddsprod_none_p_kernel(tc, x_words, x_scales, w1, gn, w2, of
                 scale_win[e:P:2, :].bitcast(I32),
                 scale_rows[e].unsqueeze(1).to_broadcast([8, 8, T // 4]),
             )
-        word_win = keep.tile([P, T], U32, name="word_win", tag="slot_b")
+        n2_t = load_list(n2, "n2_t")
+        w1_raw = keep.tile([P, PACK, 512], F32, name="w1_raw", tag="slot_b")
+        nc.sync.dma_start(w1_raw[:], w1.rearrange("(p j) c -> p j c", j=PACK))
+        n3_t = load_list(n3, "n3_t")
+        word_win = keep.tile([P, T], U32, name="word_win")
         nc.sync.dma_start(
             word_win[:].bitcast(I32), x_words[0].rearrange("p n r -> p (n r)").bitcast(I32)
         )
@@ -62,28 +69,24 @@ def tile_picked_hashoddsprod_none_p_kernel(tc, x_words, x_scales, w1, gn, w2, of
                 halves.append(raw)
             return halves
 
-        w1_raw = load_w(w1, "w1", ("w1a", "w1b"))
-        n2_t = load_list(n2, "n2_t")
-        n3_t = load_list(n3, "n3_t")
         n1_t = load_list(n1, "n1_t")
         gain = keep.tile([P, PACK], F32, name="gain")
-        nc.sync.dma_start(gain[:], gn.rearrange("(p t) o -> p (t o)", t=PACK))
+        nc.gpsimd.dma_start(gain[:], gn.rearrange("(p t) o -> p (t o)", t=PACK))
         n4_t = load_list(n4, "n4_t")
         n5_t = load_list(n5, "n5_t")
 
         x_plane = keep.tile([P, S], U8, name="x_plane", align_bytes=64)
         nc.vector.memset(x_plane[:].bitcast(I32), 0)
         scale_got = keep.tile([P, S], U8, name="scale_got")
-        nc.vector.tensor_copy(scale_got[:], scale_win[:].indirect(offs_t[:]))
-        nc.scalar.dma_start(x_plane[0:112, :].bitcast(I32), scale_got[14:126, :].bitcast(I32))
-        x_codes = keep.tile([P, S], U32, name="x_codes", align_bytes=64)
-        nc.vector.tensor_copy(x_codes[:], word_win[:].indirect(offs_t[:]))
+        for h in range(2):
+            nc.vector.tensor_copy(scale_got[:, cols(h)], scale_win[:].indirect(half_of(offs_t, h)))
+            nc.scalar.dma_start(
+                x_plane[0:112, cols(h)].bitcast(I32), scale_got[14:126, cols(h)].bitcast(I32)
+            )
 
-        w2_raw = load_w(w2, "w2", ("slot_a", "slot_b"))
-
-        def deal(raw, grouped, c, copy):
-            dst = grouped[:].rearrange("p (t m j) -> p m j t", t=PACK, j=PACK)[:, 64 * c : 64 * (c + 1), :, :]
-            copy(dst, raw[:].rearrange("p j (m t) -> p m j t", t=PACK))
+        def deal(raw, grouped, ms, ts, copy):
+            dst = grouped[:].rearrange("p (t m j) -> p m t j", t=PACK, j=PACK)[:, ms, ts, :]
+            copy(dst, raw[:].rearrange("p j (m t) -> p m t j", t=PACK)[:, :, ts, :])
 
         def mx_tiles(name):
             codes = keep.tile([P, 512], U32, name=f"{name}_codes", align_bytes=64)
@@ -91,35 +94,62 @@ def tile_picked_hashoddsprod_none_p_kernel(tc, x_words, x_scales, w1, gn, w2, of
             return codes, scales
 
         w1_bf = keep.tile([P, 2048], BF16, name="w1_bf", align_bytes=64)
-        deal(w1_raw[0], w1_bf, 0, nc.scalar.copy)
-        deal(w1_raw[1], w1_bf, 1, nc.vector.tensor_copy)
+        deal(w1_raw, w1_bf, slice(0, P), slice(0, 2), nc.vector.tensor_copy)
+        deal(w1_raw, w1_bf, slice(0, P), slice(2, 4), nc.scalar.copy)
         w1_codes, w1_scales = mx_tiles("w1")
+        nc.vector.quantize_mx(w1_codes[:, :256].bitcast(FP8X4), w1_scales[:, :256], w1_bf[:, :1024])
+        w2_raw = load_w(w2, "w2", ("slot_a", "slot_b"))
 
-        y_ps = []
-        for t in range(PACK):
+        x_codes = keep.tile([P, S], U32, name="x_codes", align_bytes=64)
+        for h in range(2):
+            nc.vector.tensor_copy(x_codes[:, cols(h)], word_win[:].indirect(half_of(offs_t, h)))
+        nc.vector.quantize_mx(w1_codes[:, 256:].bitcast(FP8X4), w1_scales[:, 256:], w1_bf[:, 1024:])
+
+        def first_product(t, dst, jc):
             m = slice(P * t, P * (t + 1))
-            nc.vector.quantize_mx(
-                w1_codes[:, m].bitcast(FP8X4), w1_scales[:, m], w1_bf[:, 512 * t : 512 * (t + 1)]
-            )
-            y = psum.tile([P, S], F32, name=f"y{t}")
             nc.tensor.matmul_mx(
-                y[:], lhsT=w1_codes[:, m].bitcast(FP8X4), lhsT_scale=w1_scales[:, m],
-                rhs=x_codes[:].bitcast(FP8X4), rhs_scale=x_plane[:], start=True, stop=True,
+                dst, lhsT=w1_codes[:, m].bitcast(FP8X4), lhsT_scale=w1_scales[:, m],
+                rhs=x_codes[:, jc].bitcast(FP8X4), rhs_scale=x_plane[:, jc], start=True, stop=True,
             )
-            y_ps.append(y)
+
+        EARLY = (0, 1)
+        y_parts = {t: [] for t in range(PACK)}
+        for h in range(2):
+            for t in EARLY:
+                y = psum.tile([P, HALF], F32, name=f"y{t}_{h}", tag=(f"h{t}", f"y{t}")[h])
+                first_product(t, y[:], cols(h))
+                y_parts[t].append((y, cols(h)))
+        for t in range(len(EARLY), PACK):
+            y = psum.tile([P, S], F32, name=f"y{t}")
+            first_product(t, y[:], slice(0, S))
+            y_parts[t].append((y, slice(0, S)))
 
         N2_ON_ACT = (1, 2, 3)
-        N1_ON_ACT = (2, 3)
+        N1_ON_ACT = (3,)
         ex, twin, half_y = {}, {}, {}
         for t in range(PACK):
             ex[t] = keep.tile([P, S], F32, name=f"ex{t}")
-            nc.scalar.activation(ex[t][:], y_ps[t][:], ACT.Exp, scale=0.5)
+            if t in N2_ON_ACT:
+                half_y[t] = keep.tile([P, S], F32, name=f"half_y{t}")
+
+        def exp_out(t, k):
+            y, jc = y_parts[t][k]
+            nc.scalar.activation(ex[t][:, jc], y[:], ACT.Exp, scale=0.5)
+
+        def halve_out(t, k):
+            y, jc = y_parts[t][k]
+            nc.scalar.activation(half_y[t][:, jc], y[:], ACT.Copy, scale=0.5)
+
+        for t in EARLY:
+            exp_out(t, 0)
+        for t in range(PACK):
+            exp_out(t, len(y_parts[t]) - 1)
             if t not in N1_ON_ACT:
                 twin[t] = keep.tile([P, S], F32, name=f"twin{t}")
                 nc.sync.dma_start(twin[t][:], ex[t][:])
             if t in N2_ON_ACT:
-                half_y[t] = keep.tile([P, S], F32, name=f"half_y{t}")
-                nc.scalar.activation(half_y[t][:], y_ps[t][:], ACT.Copy, scale=0.5)
+                for k in range(len(y_parts[t])):
+                    halve_out(t, k)
 
         num = [keep.tile([P, PACK, HALF], F32, name=f"num{h}") for h in range(2)]
         den = [keep.tile([P, PACK, HALF], F32, name=f"den{h}") for h in range(2)]
@@ -145,11 +175,11 @@ def tile_picked_hashoddsprod_none_p_kernel(tc, x_words, x_scales, w1, gn, w2, of
 
         w2_bf = keep.tile([P, 2048], BF16, name="w2_bf", align_bytes=64)
         w2_codes, w2_scales = mx_tiles("w2")
-        deal(w2_raw[0], w2_bf, 0, nc.vector.tensor_copy)
+        deal(w2_raw[0], w2_bf, slice(0, 64), slice(0, 4), nc.vector.tensor_copy)
         for h in range(2):
             g2[h, 0] = keep.tile([P, HALF], F32, name=f"g2_{h}0")
             nc.vector.tensor_copy(g2[h, 0][:], ex[0][:].indirect(half_of(n2_t, h)))
-        deal(w2_raw[1], w2_bf, 1, nc.vector.tensor_copy)
+        deal(w2_raw[1], w2_bf, slice(64, P), slice(0, 4), nc.vector.tensor_copy)
         for h in range(2):
             make_den(h, 0)
         nc.vector.quantize_mx(w2_codes[:].bitcast(FP8X4), w2_scales[:], w2_bf[:])
@@ -157,7 +187,8 @@ def tile_picked_hashoddsprod_none_p_kernel(tc, x_words, x_scales, w1, gn, w2, of
             make_num(h, 0)
             for t in range(1, PACK):
                 make_den(h, t)
-                make_num(h, t)
+                if (h, t) != (1, PACK - 1):
+                    make_num(h, t)
 
         z_codes, z_scales = mx_tiles("z")
         h_ps = [psum.tile([P, S], F32, name=f"h{t}") for t in range(PACK)]
@@ -169,21 +200,25 @@ def tile_picked_hashoddsprod_none_p_kernel(tc, x_words, x_scales, w1, gn, w2, of
         def logs(c):
             h, part = divmod(c, 2)
             pc = slice(Q * part, Q * (part + 1))
-            ln_num[c] = keep.tile([P, PACK, Q], F32, name=f"ln_num{c}")
-            ln_den[c] = keep.tile([P, PACK, Q], F32, name=f"ln_den{c}")
-            nc.scalar.activation(ln_den[c][:], den[h][:, :, pc], ACT.Ln)
-            nc.scalar.activation(ln_num[c][:], num[h][:, :, pc], ACT.Ln)
+            ln_num[c] = keep.tile([P, Q, PACK], F32, name=f"ln_num{c}")
+            ln_den[c] = keep.tile([P, Q, PACK], F32, name=f"ln_den{c}")
+            for dst, src in ((ln_den[c], den[h]), (ln_num[c], num[h])):
+                nc.scalar.activation(
+                    dst[:].rearrange("p (c i) t -> p c t i", i=4),
+                    src[:, :, pc].rearrange("p t (c i) -> p c t i", i=4),
+                    ACT.Ln,
+                )
 
         def subtract(c):
-            odds[c] = keep.tile([P, PACK, Q], F32, name=f"odds{c}")
+            odds[c] = keep.tile([P, Q, PACK], F32, name=f"odds{c}")
             nc.vector.tensor_tensor(odds[c][:], ln_num[c][:], ln_den[c][:], ALU.subtract)
 
         def scale(c):
             z_bf[c] = keep.tile([P, Q, PACK], BF16, name=f"z_bf{c}", align_bytes=64)
             nc.vector.tensor_tensor(
-                z_bf[c][:].rearrange("p (c i) t -> p c t i", i=4),
-                odds[c][:].rearrange("p t (c i) -> p c t i", i=4),
-                gain[:].unsqueeze(1).unsqueeze(3).to_broadcast([P, Q // 4, PACK, 4]),
+                z_bf[c][:],
+                odds[c][:],
+                gain[:].unsqueeze(1).to_broadcast([P, Q, PACK]),
                 ALU.mult,
             )
 
@@ -208,15 +243,17 @@ def tile_picked_hashoddsprod_none_p_kernel(tc, x_words, x_scales, w1, gn, w2, of
                 if t == 0 and c == last:
                     nc.scalar.copy(hs[0][:, zc], dst)
 
+        logs(0)
+        logs(1)
+        subtract(0)
+        make_num(1, PACK - 1)
+        logs(2)
+        logs(3)
         for c in range(chunks):
-            logs(c)
-        for step in range(chunks + 2):
-            if step < chunks:
-                subtract(step)
-            if 2 <= step:
-                project(step - 2)
-            if 1 <= step <= chunks:
-                scale(step - 1)
+            scale(c)
+            if c < last:
+                subtract(c + 1)
+            project(c)
 
         out_rows = out.rearrange("(p t) j -> p t j", t=PACK)
         for t in range(PACK):
@@ -226,9 +263,12 @@ def tile_picked_hashoddsprod_none_p_kernel(tc, x_words, x_scales, w1, gn, w2, of
             for h in range(2):
                 nc.vector.tensor_copy(g4[:, cols(h)], hs[t][:].indirect(half_of(n4_t, h)))
             res = keep.tile([P, S], F32, name=f"res{t}")
-            for h in range(2):
-                nc.vector.tensor_tensor(res[:, cols(h)], hs[t][:].indirect(half_of(n5_t, h)), g4[:, cols(h)], ALU.mult)
+            bounds = (0, HALF, HALF + Q, S) if t == PACK - 1 else (0, HALF, S)
+            for lo, hi in zip(bounds, bounds[1:]):
+                nc.vector.tensor_tensor(
+                    res[:, lo:hi], hs[t][:].indirect(n5_t[:, lo // 16 : hi // 16]), g4[:, lo:hi], ALU.mult
+                )
                 if t == PACK - 1:
-                    nc.sync.dma_start(out_rows[:, t, cols(h)], res[:, cols(h)])
+                    nc.sync.dma_start(out_rows[:, t, lo:hi], res[:, lo:hi])
             if t < PACK - 1:
                 nc.sync.dma_start(out_rows[:, t, :], res[:])

@@ -17,9 +17,16 @@ ACT = mybir.ActivationFunctionType
 
 P = 128
 PACK = 4
+GROUP = 16
+RUNS = P // GROUP
+BLOCK_ROWS = 8
 HALF = S // 2
-LCOLS = HALF // 16
-Q = 128
+CHUNK = 128
+VECTOR_TILES = (0, 1)
+SCALAR_TILES = (2, 3)
+LAST = PACK - 1
+SHIFT = GROUP - 2
+SHIFTED = P - GROUP
 
 
 def tile_picked_hashoddsprod_none_p_kernel(tc, x_words, x_scales, w1, gn, w2, offs, n1, n2, n3, n4, n5, out):
@@ -29,246 +36,235 @@ def tile_picked_hashoddsprod_none_p_kernel(tc, x_words, x_scales, w1, gn, w2, of
         psum = ctx.enter_context(tc.psum_pool(name="psum", bufs=1))
 
         def load_list(src, name):
-            tile = keep.tile([P, S // 16], U16, name=name)
+            tile = keep.tile([P, S // GROUP], U16, name=name)
             nc.sync.dma_start(tile[:], src)
             return tile
 
-        def half_of(tile, h):
-            return tile[:, h * LCOLS : (h + 1) * LCOLS]
+        def entries(list_tile, lo, hi):
+            return list_tile[:, lo // GROUP : hi // GROUP]
 
-        def cols(h):
-            return slice(h * HALF, (h + 1) * HALF)
+        def mx_tiles(name, width, codes_tag):
+            codes = keep.tile([P, width], U32, name=f"{name}_codes", tag=codes_tag, align_bytes=64)
+            scales = keep.tile([P, width], U8, name=f"{name}_scales", align_bytes=64)
+            return codes, scales
 
-        warm = keep.tile([P, 2], F32, name="warm")
-        nc.vector.memset(warm[:, 0:1], 0.0)
-        nc.scalar.activation(warm[:, 1:2], warm[:, 0:1], ACT.Exp)
-        offs_t = load_list(offs, "offs_t")
-        scale_win = keep.tile([P, T], U8, name="scale_win", tag="slot_a")
+        def product(dst, w_codes, w_scales, place, codes, scales, cols):
+            rows = slice(P * place, P * (place + 1))
+            nc.tensor.matmul_mx(
+                dst,
+                lhsT=w_codes[:, rows].bitcast(FP8X4),
+                lhsT_scale=w_scales[:, rows],
+                rhs=codes[:, cols].bitcast(FP8X4),
+                rhs_scale=scales[:, cols],
+                start=True,
+                stop=True,
+            )
+
+        halves = (slice(0, HALF), slice(HALF, S))
+
+        window = [keep.tile([P, 2 * S], F32, name=f"window{t}") for t in range(PACK)]
+        half_y = {t: keep.tile([P, 2 * S], F32, name=f"half_y{t}") for t in SCALAR_TILES}
+        padded = window + [half_y[t] for t in SCALAR_TILES]
+        for tile in padded[:-1]:
+            nc.gpsimd.memset(tile[:, S:], 0.0)
+        nc.scalar.copy(padded[-1][:, S:], padded[0][:, S:])
+
+        offs_list = load_list(offs, "offs_list")
+        scale_window = keep.tile([P, T], U8, name="scale_window", tag="scale_window_then_w2")
         scale_rows = x_scales[0].bitcast(I32).rearrange("(g e) c -> e g c", e=2)
         for e in range(2):
             nc.sync.dma_start(
-                scale_win[e:P:2, :].bitcast(I32),
-                scale_rows[e].unsqueeze(1).to_broadcast([8, 8, T // 4]),
+                scale_window[e:P:2, :].bitcast(I32),
+                scale_rows[e].unsqueeze(1).to_broadcast([RUNS, GROUP // 2, T // 4]),
             )
-        n2_t = load_list(n2, "n2_t")
-        w1_raw = keep.tile([P, PACK, 512], F32, name="w1_raw", tag="slot_b")
-        nc.sync.dma_start(w1_raw[:], w1.rearrange("(p j) c -> p j c", j=PACK))
-        n3_t = load_list(n3, "n3_t")
-        word_win = keep.tile([P, T], U32, name="word_win")
-        nc.sync.dma_start(
-            word_win[:].bitcast(I32), x_words[0].rearrange("p n r -> p (n r)").bitcast(I32)
-        )
-
-        def load_w(w, name, tags):
-            halves = []
-            for c in range(2):
-                raw = keep.tile([P, PACK, 256], F32, name=f"{name}_raw{c}", tag=tags[c])
-                nc.sync.dma_start(
-                    raw[:], w.rearrange("(p j) c -> p j c", j=PACK)[:, :, 256 * c : 256 * (c + 1)]
-                )
-                halves.append(raw)
-            return halves
-
-        n1_t = load_list(n1, "n1_t")
-        gain = keep.tile([P, PACK], F32, name="gain")
-        nc.gpsimd.dma_start(gain[:], gn.rearrange("(p t) o -> p (t o)", t=PACK))
-        n4_t = load_list(n4, "n4_t")
-        n5_t = load_list(n5, "n5_t")
+        n2_list = load_list(n2, "n2_list")
+        w1_raw = keep.tile([P, PACK, H], F32, name="w1_raw")
+        nc.sync.dma_start(w1_raw[:], w1.rearrange("(p j) i -> p j i", j=PACK))
+        n3_list = load_list(n3, "n3_list")
+        word_window = keep.tile([P, T], U32, name="word_window")
+        nc.sync.dma_start(word_window[:].bitcast(I32), x_words[0].rearrange("p n r -> p (n r)").bitcast(I32))
+        n1_list = load_list(n1, "n1_list")
+        n4_list = load_list(n4, "n4_list")
+        n5_list = load_list(n5, "n5_list")
 
         x_plane = keep.tile([P, S], U8, name="x_plane", align_bytes=64)
         nc.vector.memset(x_plane[:].bitcast(I32), 0)
-        scale_got = keep.tile([P, S], U8, name="scale_got")
-        for h in range(2):
-            nc.vector.tensor_copy(scale_got[:, cols(h)], scale_win[:].indirect(half_of(offs_t, h)))
+        picked_scales = keep.tile([P, S], U8, name="picked_scales", tag="picked_scales_then_gain")
+        for cols in halves:
+            nc.vector.tensor_copy(
+                picked_scales[:, cols], scale_window[:].indirect(entries(offs_list, cols.start, cols.stop))
+            )
             nc.scalar.dma_start(
-                x_plane[0:112, cols(h)].bitcast(I32), scale_got[14:126, cols(h)].bitcast(I32)
+                x_plane[0:SHIFTED, cols].bitcast(I32), picked_scales[SHIFT : SHIFT + SHIFTED, cols].bitcast(I32)
             )
 
-        def deal(raw, grouped, ms, ts, copy):
-            dst = grouped[:].rearrange("p (t m j) -> p m t j", t=PACK, j=PACK)[:, ms, ts, :]
-            copy(dst, raw[:].rearrange("p j (m t) -> p m t j", t=PACK)[:, :, ts, :])
+        w1_bf = keep.tile([P, PACK * H], BF16, name="w1_bf", align_bytes=64)
+        w1_dealt = w1_bf[:].rearrange("p (t m j) -> p m t j", t=PACK, j=PACK)
+        w1_source = w1_raw[:].rearrange("p j (m t) -> p m t j", t=PACK)
+        nc.vector.tensor_copy(w1_dealt[:, :, :2, :], w1_source[:, :, :2, :])
+        nc.scalar.copy(w1_dealt[:, :, 2:, :], w1_source[:, :, 2:, :])
+        w1_codes, w1_scales = mx_tiles("w1", H, "w1_codes")
+        for cols in halves:
+            nc.vector.quantize_mx(
+                w1_codes[:, cols].bitcast(FP8X4), w1_scales[:, cols], w1_bf[:, PACK * cols.start : PACK * cols.stop]
+            )
 
-        def mx_tiles(name):
-            codes = keep.tile([P, 512], U32, name=f"{name}_codes", align_bytes=64)
-            scales = keep.tile([P, 512], U8, name=f"{name}_scales", align_bytes=64)
-            return codes, scales
-
-        w1_bf = keep.tile([P, 2048], BF16, name="w1_bf", align_bytes=64)
-        deal(w1_raw, w1_bf, slice(0, P), slice(0, 2), nc.vector.tensor_copy)
-        deal(w1_raw, w1_bf, slice(0, P), slice(2, 4), nc.scalar.copy)
-        w1_codes, w1_scales = mx_tiles("w1")
-        nc.vector.quantize_mx(w1_codes[:, :256].bitcast(FP8X4), w1_scales[:, :256], w1_bf[:, :1024])
-        w2_raw = load_w(w2, "w2", ("slot_a", "slot_b"))
+        w2_raw = keep.tile([P, 2, PACK, HALF], F32, name="w2_raw", tag="scale_window_then_w2")
+        for c, cols in enumerate(halves):
+            nc.sync.dma_start(w2_raw[:, c], w2.rearrange("(p j) m -> p j m", j=PACK)[:, :, cols])
 
         x_codes = keep.tile([P, S], U32, name="x_codes", align_bytes=64)
-        for h in range(2):
-            nc.vector.tensor_copy(x_codes[:, cols(h)], word_win[:].indirect(half_of(offs_t, h)))
-        nc.vector.quantize_mx(w1_codes[:, 256:].bitcast(FP8X4), w1_scales[:, 256:], w1_bf[:, 1024:])
+        for cols in halves:
+            nc.vector.tensor_copy(x_codes[:, cols], word_window[:].indirect(entries(offs_list, cols.start, cols.stop)))
 
-        def first_product(t, dst, jc):
-            m = slice(P * t, P * (t + 1))
-            nc.tensor.matmul_mx(
-                dst, lhsT=w1_codes[:, m].bitcast(FP8X4), lhsT_scale=w1_scales[:, m],
-                rhs=x_codes[:, jc].bitcast(FP8X4), rhs_scale=x_plane[:, jc], start=True, stop=True,
+        y_half = {}
+        for c, cols in enumerate(halves):
+            for t in VECTOR_TILES:
+                y_half[t, c] = psum.tile([P, HALF], F32, name=f"y{t}_{c}", tag=(f"h{t}", f"y{t}")[c])
+                product(y_half[t, c][:], w1_codes, w1_scales, t, x_codes, x_plane, cols)
+        y_whole = {}
+        for t in SCALAR_TILES:
+            y_whole[t] = psum.tile([P, S], F32, name=f"y{t}")
+            product(y_whole[t][:], w1_codes, w1_scales, t, x_codes, x_plane, slice(0, S))
+
+        ex_copy = {}
+        for t in VECTOR_TILES:
+            nc.scalar.activation(window[t][:, halves[0]], y_half[t, 0][:], ACT.Exp, scale=0.5)
+        for t in VECTOR_TILES:
+            nc.scalar.activation(window[t][:, halves[1]], y_half[t, 1][:], ACT.Exp, scale=0.5)
+            ex_copy[t] = keep.tile([P, S], F32, name=f"ex_copy{t}")
+            nc.sync.dma_start(ex_copy[t][:], window[t][:, :S])
+        for t in SCALAR_TILES:
+            nc.scalar.activation(window[t][:, :S], y_whole[t][:], ACT.Exp, scale=0.5)
+            nc.scalar.activation(half_y[t][:, :S], y_whole[t][:], ACT.Copy, scale=0.5)
+
+        gain = keep.tile([P, PACK], F32, name="gain", tag="picked_scales_then_gain")
+        nc.sync.dma_start(gain[:], gn.rearrange("(p t) o -> p (t o)", t=PACK))
+
+        num = keep.tile([P, PACK, S], F32, name="num")
+        den = keep.tile([P, PACK, S], F32, name="den")
+        ex_n1, ex_n2 = {}, {}
+        for t in SCALAR_TILES:
+            ex_n2[t] = keep.tile([P, S], F32, name=f"ex_n2_{t}")
+            nc.scalar.activation(ex_n2[t][:], half_y[t][:].indirect(n2_list[:]), ACT.Exp)
+            ex_n1[t] = keep.tile([P, S], F32, name=f"ex_n1_{t}")
+            nc.scalar.activation(ex_n1[t][:], half_y[t][:].indirect(n1_list[:]), ACT.Exp)
+
+        w2_bf = keep.tile([P, PACK * N], BF16, name="w2_bf", align_bytes=64)
+        w2_dealt = w2_bf[:].rearrange("p (t b rj) -> p b t rj", t=PACK, rj=BLOCK_ROWS * PACK)
+        blocks = HALF // (BLOCK_ROWS * PACK)
+        for c in range(2):
+            nc.gpsimd.tensor_scalar(
+                w2_dealt[:, blocks * c : blocks * (c + 1)],
+                w2_raw[:, c].rearrange("p j (u r) -> p u r j", r=BLOCK_ROWS),
+                1.0,
+                0.0,
+                ALU.mult,
+                ALU.add,
+            )
+        w2_codes, w2_scales = mx_tiles("w2", P, "w2_codes")
+
+        def gather_den(t, lo, hi):
+            nc.vector.tensor_tensor(
+                den[:, t, lo:hi], window[t][:].indirect(entries(n3_list, lo, hi)), ex_n2[t][:, lo:hi], ALU.add
             )
 
-        EARLY = (0, 1)
-        y_parts = {t: [] for t in range(PACK)}
-        for h in range(2):
-            for t in EARLY:
-                y = psum.tile([P, HALF], F32, name=f"y{t}_{h}", tag=(f"h{t}", f"y{t}")[h])
-                first_product(t, y[:], cols(h))
-                y_parts[t].append((y, cols(h)))
-        for t in range(len(EARLY), PACK):
-            y = psum.tile([P, S], F32, name=f"y{t}")
-            first_product(t, y[:], slice(0, S))
-            y_parts[t].append((y, slice(0, S)))
+        def add_num(t, lo, hi):
+            nc.vector.tensor_tensor(num[:, t, lo:hi], ex_n1[t][:, lo:hi], window[t][:, lo:hi], ALU.add)
 
-        N2_ON_ACT = (1, 2, 3)
-        N1_ON_ACT = (3,)
-        ex, twin, half_y = {}, {}, {}
-        for t in range(PACK):
-            ex[t] = keep.tile([P, S], F32, name=f"ex{t}")
-            if t in N2_ON_ACT:
-                half_y[t] = keep.tile([P, S], F32, name=f"half_y{t}")
+        for t in VECTOR_TILES:
+            ex_n2[t] = keep.tile([P, S], F32, name=f"ex_n2_{t}")
+            nc.vector.tensor_copy(ex_n2[t][:], window[t][:].indirect(n2_list[:]))
+        for t in VECTOR_TILES:
+            gather_den(t, 0, S)
+        for t in VECTOR_TILES:
+            nc.vector.tensor_tensor(num[:, t, :], window[t][:].indirect(n1_list[:]), ex_copy[t][:], ALU.add)
+        for t in SCALAR_TILES:
+            gather_den(t, 0, HALF)
+            add_num(t, 0, HALF)
+        nc.vector.quantize_mx(w2_codes[:].bitcast(FP8X4), w2_scales[:], w2_bf[:, : PACK * P])
+        for t in SCALAR_TILES:
+            gather_den(t, HALF, S)
+            if t < LAST:
+                add_num(t, HALF, S)
 
-        def exp_out(t, k):
-            y, jc = y_parts[t][k]
-            nc.scalar.activation(ex[t][:, jc], y[:], ACT.Exp, scale=0.5)
+        z_codes, z_scales = mx_tiles("z", S, "z_codes")
+        h_bank = [psum.tile([P, S], F32, name=f"h{t}") for t in range(PACK)]
+        chunks = S // CHUNK
+        last_chunk = chunks - 1
+        ln_num, ln_den, log_odds, z_bf = {}, {}, {}, {}
 
-        def halve_out(t, k):
-            y, jc = y_parts[t][k]
-            nc.scalar.activation(half_y[t][:, jc], y[:], ACT.Copy, scale=0.5)
-
-        for t in EARLY:
-            exp_out(t, 0)
-        for t in range(PACK):
-            exp_out(t, len(y_parts[t]) - 1)
-            if t not in N1_ON_ACT:
-                twin[t] = keep.tile([P, S], F32, name=f"twin{t}")
-                nc.sync.dma_start(twin[t][:], ex[t][:])
-            if t in N2_ON_ACT:
-                for k in range(len(y_parts[t])):
-                    halve_out(t, k)
-
-        num = [keep.tile([P, PACK, HALF], F32, name=f"num{h}") for h in range(2)]
-        den = [keep.tile([P, PACK, HALF], F32, name=f"den{h}") for h in range(2)]
-        g1, g2 = {}, {}
-        for h in range(2):
-            for t in N2_ON_ACT:
-                g2[h, t] = keep.tile([P, HALF], F32, name=f"g2_{h}{t}")
-                nc.scalar.activation(g2[h, t][:], half_y[t][:].indirect(half_of(n2_t, h)), ACT.Exp)
-                if t in N1_ON_ACT:
-                    g1[h, t] = keep.tile([P, HALF], F32, name=f"g1_{h}{t}")
-                    nc.scalar.activation(g1[h, t][:], half_y[t][:].indirect(half_of(n1_t, h)), ACT.Exp)
-
-        def make_den(h, t):
-            nc.vector.tensor_tensor(den[h][:, t, :], ex[t][:].indirect(half_of(n3_t, h)), g2[h, t][:], ALU.add)
-
-        def make_num(h, t):
-            if t in N1_ON_ACT:
-                nc.vector.tensor_tensor(num[h][:, t, :], g1[h, t][:], ex[t][:, cols(h)], ALU.add)
-            else:
-                nc.vector.tensor_tensor(
-                    num[h][:, t, :], ex[t][:].indirect(half_of(n1_t, h)), twin[t][:, cols(h)], ALU.add
-                )
-
-        w2_bf = keep.tile([P, 2048], BF16, name="w2_bf", align_bytes=64)
-        w2_codes, w2_scales = mx_tiles("w2")
-        deal(w2_raw[0], w2_bf, slice(0, 64), slice(0, 4), nc.vector.tensor_copy)
-        for h in range(2):
-            g2[h, 0] = keep.tile([P, HALF], F32, name=f"g2_{h}0")
-            nc.vector.tensor_copy(g2[h, 0][:], ex[0][:].indirect(half_of(n2_t, h)))
-        deal(w2_raw[1], w2_bf, slice(64, P), slice(0, 4), nc.vector.tensor_copy)
-        for h in range(2):
-            make_den(h, 0)
-        nc.vector.quantize_mx(w2_codes[:].bitcast(FP8X4), w2_scales[:], w2_bf[:])
-        for h in range(2):
-            make_num(h, 0)
-            for t in range(1, PACK):
-                make_den(h, t)
-                if (h, t) != (1, PACK - 1):
-                    make_num(h, t)
-
-        z_codes, z_scales = mx_tiles("z")
-        h_ps = [psum.tile([P, S], F32, name=f"h{t}") for t in range(PACK)]
-        hs = [keep.tile([P, S], F32, name=f"hs{t}") for t in range(PACK)]
-        chunks = S // Q
-        last = chunks - 1
-        ln_num, ln_den, odds, z_bf = {}, {}, {}, {}
-
-        def logs(c):
-            h, part = divmod(c, 2)
-            pc = slice(Q * part, Q * (part + 1))
-            ln_num[c] = keep.tile([P, Q, PACK], F32, name=f"ln_num{c}")
-            ln_den[c] = keep.tile([P, Q, PACK], F32, name=f"ln_den{c}")
-            for dst, src in ((ln_den[c], den[h]), (ln_num[c], num[h])):
+        def logarithms(c):
+            ln_num[c] = keep.tile([P, CHUNK, PACK], F32, name=f"ln_num{c}")
+            ln_den[c] = keep.tile([P, CHUNK, PACK], F32, name=f"ln_den{c}")
+            for dst, src in ((ln_den[c], den), (ln_num[c], num)):
                 nc.scalar.activation(
-                    dst[:].rearrange("p (c i) t -> p c t i", i=4),
-                    src[:, :, pc].rearrange("p t (c i) -> p c t i", i=4),
+                    dst[:].rearrange("p (u v) t -> p u t v", v=4),
+                    src[:, :, CHUNK * c : CHUNK * (c + 1)].rearrange("p t (u v) -> p u t v", v=4),
                     ACT.Ln,
                 )
 
         def subtract(c):
-            odds[c] = keep.tile([P, Q, PACK], F32, name=f"odds{c}")
-            nc.vector.tensor_tensor(odds[c][:], ln_num[c][:], ln_den[c][:], ALU.subtract)
+            log_odds[c] = keep.tile([P, CHUNK, PACK], F32, name=f"log_odds{c}")
+            nc.vector.tensor_tensor(log_odds[c][:], ln_num[c][:], ln_den[c][:], ALU.subtract)
 
-        def scale(c):
-            z_bf[c] = keep.tile([P, Q, PACK], BF16, name=f"z_bf{c}", align_bytes=64)
+        def apply_gain(c):
+            z_bf[c] = keep.tile([P, CHUNK, PACK], BF16, name=f"z_bf{c}", tag=f"z_bf{c}", align_bytes=64)
             nc.vector.tensor_tensor(
-                z_bf[c][:],
-                odds[c][:],
-                gain[:].unsqueeze(1).to_broadcast([P, Q, PACK]),
-                ALU.mult,
+                z_bf[c][:], log_odds[c][:], gain[:].unsqueeze(1).to_broadcast([P, CHUNK, PACK]), ALU.mult
             )
 
         def project(c):
-            zc = slice(Q * c, Q * (c + 1))
+            cols = slice(CHUNK * c, CHUNK * (c + 1))
             nc.vector.quantize_mx(
-                z_codes[:, zc].bitcast(FP8X4), z_scales[:, zc], z_bf[c][:].rearrange("p c t -> p (c t)")
+                z_codes[:, cols].bitcast(FP8X4), z_scales[:, cols], z_bf[c][:].rearrange("p u t -> p (u t)")
             )
-            for t in range(PACK):
-                m = slice(P * t, P * (t + 1))
-                if t == 0 and c == last:
-                    h0_end = psum.tile([P, Q], F32, name="y0")
-                    dst = h0_end[:]
-                else:
-                    dst = h_ps[t][:, zc]
-                nc.tensor.matmul_mx(
-                    dst, lhsT=w2_codes[:, m].bitcast(FP8X4), lhsT_scale=w2_scales[:, m],
-                    rhs=z_codes[:, zc].bitcast(FP8X4), rhs_scale=z_scales[:, zc], start=True, stop=True,
-                )
-                if t == 0 and c == last - 1:
-                    nc.scalar.copy(hs[0][:, : Q * last], h_ps[0][:, : Q * last])
-                if t == 0 and c == last:
-                    nc.scalar.copy(hs[0][:, zc], dst)
+            if c == last_chunk:
+                h0_end = psum.tile([P, CHUNK], F32, name="h0_end", tag="y0")
+                product(h0_end[:], w2_codes, w2_scales, 0, z_codes, z_scales, cols)
+                nc.scalar.copy(window[0][:, cols], h0_end[:])
+            else:
+                product(h_bank[0][:, cols], w2_codes, w2_scales, 0, z_codes, z_scales, cols)
+            if c == last_chunk - 1:
+                nc.scalar.copy(window[0][:, : cols.stop], h_bank[0][:, : cols.stop])
 
-        logs(0)
-        logs(1)
+        for c in range(chunks // 2):
+            logarithms(c)
         subtract(0)
-        make_num(1, PACK - 1)
-        logs(2)
-        logs(3)
+        add_num(LAST, HALF, S)
+        for c in range(chunks // 2, chunks):
+            logarithms(c)
         for c in range(chunks):
-            scale(c)
-            if c < last:
+            apply_gain(c)
+            if c < last_chunk:
                 subtract(c + 1)
             project(c)
 
-        out_rows = out.rearrange("(p t) j -> p t j", t=PACK)
-        for t in range(PACK):
+        rest_codes, rest_scales = mx_tiles("w2_rest", LAST * P, f"z_bf{last_chunk}")
+        for lo, hi in ((0, P), (P, LAST * P)):
+            nc.vector.quantize_mx(
+                rest_codes[:, lo:hi].bitcast(FP8X4), rest_scales[:, lo:hi], w2_bf[:, PACK * (P + lo) : PACK * (P + hi)]
+            )
+        for t in range(1, PACK):
+            product(h_bank[t][:], rest_codes, rest_scales, t - 1, z_codes, z_scales, slice(0, S))
+
+        out_rows = out.rearrange("(b t r) j -> t b r j", t=PACK, r=BLOCK_ROWS)
+        h_n4 = {}
+
+        def gather_n4(t):
             if t > 0:
-                nc.scalar.copy(hs[t][:], h_ps[t][:])
-            g4 = keep.tile([P, S], F32, name=f"g4_{t}")
-            for h in range(2):
-                nc.vector.tensor_copy(g4[:, cols(h)], hs[t][:].indirect(half_of(n4_t, h)))
-            res = keep.tile([P, S], F32, name=f"res{t}")
-            bounds = (0, HALF, HALF + Q, S) if t == PACK - 1 else (0, HALF, S)
+                nc.scalar.copy(window[t][:, :S], h_bank[t][:])
+            h_n4[t] = keep.tile([P, S], F32, name=f"h_n4_{t}")
+            nc.vector.tensor_copy(h_n4[t][:], window[t][:].indirect(n4_list[:]))
+
+        gather_n4(0)
+        for t in range(PACK):
+            if t < LAST:
+                gather_n4(t + 1)
+            result = keep.tile([P, S], F32, name=f"result{t}")
+            bounds = (0, HALF, HALF + CHUNK, S) if t == LAST else (0, S)
             for lo, hi in zip(bounds, bounds[1:]):
                 nc.vector.tensor_tensor(
-                    res[:, lo:hi], hs[t][:].indirect(n5_t[:, lo // 16 : hi // 16]), g4[:, lo:hi], ALU.mult
+                    result[:, lo:hi], window[t][:].indirect(entries(n5_list, lo, hi)), h_n4[t][:, lo:hi], ALU.mult
                 )
-                if t == PACK - 1:
-                    nc.sync.dma_start(out_rows[:, t, lo:hi], res[:, lo:hi])
-            if t < PACK - 1:
-                nc.sync.dma_start(out_rows[:, t, :], res[:])
+                nc.sync.dma_start(out_rows[t][:, :, lo:hi], result[:, lo:hi])

from contextlib import ExitStack

import concourse.mybir as mybir

K, T, S, N, H = 512, 2048, 512, 512, 512
FLOPS = 2 * K * H * S + 2 * H * N * S

F32 = mybir.dt.float32
BF16 = mybir.dt.bfloat16
I32 = mybir.dt.int32
U32 = mybir.dt.uint32
U16 = mybir.dt.uint16
U8 = mybir.dt.uint8
FP8X4 = mybir.dt.float8_e4m3fn_x4
ALU = mybir.AluOpType
ACT = mybir.ActivationFunctionType

P = 128
PACK = 4
GROUP = 16
RUNS = P // GROUP
BLOCK_ROWS = 8
HALF = S // 2
CHUNK = 128
VECTOR_TILES = (0, 1)
SCALAR_TILES = (2, 3)
LAST = PACK - 1
SHIFT = GROUP - 2
SHIFTED = P - GROUP


def tile_picked_hashoddsprod_none_p_kernel(tc, x_words, x_scales, w1, gn, w2, offs, n1, n2, n3, n4, n5, out):
    nc = tc.nc
    with ExitStack() as ctx:
        keep = ctx.enter_context(tc.tile_pool(name="keep", bufs=1))
        psum = ctx.enter_context(tc.psum_pool(name="psum", bufs=1))

        def load_list(src, name):
            tile = keep.tile([P, S // GROUP], U16, name=name)
            nc.sync.dma_start(tile[:], src)
            return tile

        def entries(list_tile, lo, hi):
            return list_tile[:, lo // GROUP : hi // GROUP]

        def mx_tiles(name, width, codes_tag):
            codes = keep.tile([P, width], U32, name=f"{name}_codes", tag=codes_tag, align_bytes=64)
            scales = keep.tile([P, width], U8, name=f"{name}_scales", align_bytes=64)
            return codes, scales

        def product(dst, w_codes, w_scales, place, codes, scales, cols):
            rows = slice(P * place, P * (place + 1))
            nc.tensor.matmul_mx(
                dst,
                lhsT=w_codes[:, rows].bitcast(FP8X4),
                lhsT_scale=w_scales[:, rows],
                rhs=codes[:, cols].bitcast(FP8X4),
                rhs_scale=scales[:, cols],
                start=True,
                stop=True,
            )

        halves = (slice(0, HALF), slice(HALF, S))

        window = [keep.tile([P, 2 * S], F32, name=f"window{t}") for t in range(PACK)]
        half_y = {t: keep.tile([P, 2 * S], F32, name=f"half_y{t}") for t in SCALAR_TILES}
        padded = window + [half_y[t] for t in SCALAR_TILES]
        for tile in padded[:-1]:
            nc.gpsimd.memset(tile[:, S:], 0.0)
        nc.scalar.copy(padded[-1][:, S:], padded[0][:, S:])

        offs_list = load_list(offs, "offs_list")
        scale_window = keep.tile([P, T], U8, name="scale_window", tag="scale_window_then_w2")
        scale_rows = x_scales[0].bitcast(I32).rearrange("(g e) c -> e g c", e=2)
        for e in range(2):
            nc.sync.dma_start(
                scale_window[e:P:2, :].bitcast(I32),
                scale_rows[e].unsqueeze(1).to_broadcast([RUNS, GROUP // 2, T // 4]),
            )
        n2_list = load_list(n2, "n2_list")
        w1_raw = keep.tile([P, PACK, H], F32, name="w1_raw")
        nc.sync.dma_start(w1_raw[:], w1.rearrange("(p j) i -> p j i", j=PACK))
        n3_list = load_list(n3, "n3_list")
        word_window = keep.tile([P, T], U32, name="word_window")
        nc.sync.dma_start(word_window[:].bitcast(I32), x_words[0].rearrange("p n r -> p (n r)").bitcast(I32))
        n1_list = load_list(n1, "n1_list")
        n4_list = load_list(n4, "n4_list")
        n5_list = load_list(n5, "n5_list")

        x_plane = keep.tile([P, S], U8, name="x_plane", align_bytes=64)
        nc.vector.memset(x_plane[:].bitcast(I32), 0)
        picked_scales = keep.tile([P, S], U8, name="picked_scales", tag="picked_scales_then_gain")
        for cols in halves:
            nc.vector.tensor_copy(
                picked_scales[:, cols], scale_window[:].indirect(entries(offs_list, cols.start, cols.stop))
            )
            nc.scalar.dma_start(
                x_plane[0:SHIFTED, cols].bitcast(I32), picked_scales[SHIFT : SHIFT + SHIFTED, cols].bitcast(I32)
            )

        w1_bf = keep.tile([P, PACK * H], BF16, name="w1_bf", align_bytes=64)
        w1_dealt = w1_bf[:].rearrange("p (t m j) -> p m t j", t=PACK, j=PACK)
        w1_source = w1_raw[:].rearrange("p j (m t) -> p m t j", t=PACK)
        nc.vector.tensor_copy(w1_dealt[:, :, :2, :], w1_source[:, :, :2, :])
        nc.scalar.copy(w1_dealt[:, :, 2:, :], w1_source[:, :, 2:, :])
        w1_codes, w1_scales = mx_tiles("w1", H, "w1_codes")
        for cols in halves:
            nc.vector.quantize_mx(
                w1_codes[:, cols].bitcast(FP8X4), w1_scales[:, cols], w1_bf[:, PACK * cols.start : PACK * cols.stop]
            )

        w2_raw = keep.tile([P, 2, PACK, HALF], F32, name="w2_raw", tag="scale_window_then_w2")
        for c, cols in enumerate(halves):
            nc.sync.dma_start(w2_raw[:, c], w2.rearrange("(p j) m -> p j m", j=PACK)[:, :, cols])

        x_codes = keep.tile([P, S], U32, name="x_codes", align_bytes=64)
        for cols in halves:
            nc.vector.tensor_copy(x_codes[:, cols], word_window[:].indirect(entries(offs_list, cols.start, cols.stop)))

        y_half = {}
        for c, cols in enumerate(halves):
            for t in VECTOR_TILES:
                y_half[t, c] = psum.tile([P, HALF], F32, name=f"y{t}_{c}", tag=(f"h{t}", f"y{t}")[c])
                product(y_half[t, c][:], w1_codes, w1_scales, t, x_codes, x_plane, cols)
        y_whole = {}
        for t in SCALAR_TILES:
            y_whole[t] = psum.tile([P, S], F32, name=f"y{t}")
            product(y_whole[t][:], w1_codes, w1_scales, t, x_codes, x_plane, slice(0, S))

        ex_copy = {}
        for t in VECTOR_TILES:
            nc.scalar.activation(window[t][:, halves[0]], y_half[t, 0][:], ACT.Exp, scale=0.5)
        for t in VECTOR_TILES:
            nc.scalar.activation(window[t][:, halves[1]], y_half[t, 1][:], ACT.Exp, scale=0.5)
            ex_copy[t] = keep.tile([P, S], F32, name=f"ex_copy{t}")
            nc.sync.dma_start(ex_copy[t][:], window[t][:, :S])
        for t in SCALAR_TILES:
            nc.scalar.activation(window[t][:, :S], y_whole[t][:], ACT.Exp, scale=0.5)
            nc.scalar.activation(half_y[t][:, :S], y_whole[t][:], ACT.Copy, scale=0.5)

        gain = keep.tile([P, PACK], F32, name="gain", tag="picked_scales_then_gain")
        nc.sync.dma_start(gain[:], gn.rearrange("(p t) o -> p (t o)", t=PACK))

        num = keep.tile([P, PACK, S], F32, name="num")
        den = keep.tile([P, PACK, S], F32, name="den")
        ex_n1, ex_n2 = {}, {}
        for t in SCALAR_TILES:
            ex_n2[t] = keep.tile([P, S], F32, name=f"ex_n2_{t}")
            nc.scalar.activation(ex_n2[t][:], half_y[t][:].indirect(n2_list[:]), ACT.Exp)
            ex_n1[t] = keep.tile([P, S], F32, name=f"ex_n1_{t}")
            nc.scalar.activation(ex_n1[t][:], half_y[t][:].indirect(n1_list[:]), ACT.Exp)

        w2_bf = keep.tile([P, PACK * N], BF16, name="w2_bf", align_bytes=64)
        w2_dealt = w2_bf[:].rearrange("p (t b rj) -> p b t rj", t=PACK, rj=BLOCK_ROWS * PACK)
        blocks = HALF // (BLOCK_ROWS * PACK)
        for c in range(2):
            nc.gpsimd.tensor_scalar(
                w2_dealt[:, blocks * c : blocks * (c + 1)],
                w2_raw[:, c].rearrange("p j (u r) -> p u r j", r=BLOCK_ROWS),
                1.0,
                0.0,
                ALU.mult,
                ALU.add,
            )
        w2_codes, w2_scales = mx_tiles("w2", P, "w2_codes")

        def gather_den(t, lo, hi):
            nc.vector.tensor_tensor(
                den[:, t, lo:hi], window[t][:].indirect(entries(n3_list, lo, hi)), ex_n2[t][:, lo:hi], ALU.add
            )

        def add_num(t, lo, hi):
            nc.vector.tensor_tensor(num[:, t, lo:hi], ex_n1[t][:, lo:hi], window[t][:, lo:hi], ALU.add)

        for t in VECTOR_TILES:
            ex_n2[t] = keep.tile([P, S], F32, name=f"ex_n2_{t}")
            nc.vector.tensor_copy(ex_n2[t][:], window[t][:].indirect(n2_list[:]))
        for t in VECTOR_TILES:
            gather_den(t, 0, S)
        for t in VECTOR_TILES:
            nc.vector.tensor_tensor(num[:, t, :], window[t][:].indirect(n1_list[:]), ex_copy[t][:], ALU.add)
        for t in SCALAR_TILES:
            gather_den(t, 0, HALF)
            add_num(t, 0, HALF)
        nc.vector.quantize_mx(w2_codes[:].bitcast(FP8X4), w2_scales[:], w2_bf[:, : PACK * P])
        for t in SCALAR_TILES:
            gather_den(t, HALF, S)
            if t < LAST:
                add_num(t, HALF, S)

        z_codes, z_scales = mx_tiles("z", S, "z_codes")
        h_bank = [psum.tile([P, S], F32, name=f"h{t}") for t in range(PACK)]
        chunks = S // CHUNK
        last_chunk = chunks - 1
        ln_num, ln_den, log_odds, z_bf = {}, {}, {}, {}

        def logarithms(c):
            ln_num[c] = keep.tile([P, CHUNK, PACK], F32, name=f"ln_num{c}")
            ln_den[c] = keep.tile([P, CHUNK, PACK], F32, name=f"ln_den{c}")
            for dst, src in ((ln_den[c], den), (ln_num[c], num)):
                nc.scalar.activation(
                    dst[:].rearrange("p (u v) t -> p u t v", v=4),
                    src[:, :, CHUNK * c : CHUNK * (c + 1)].rearrange("p t (u v) -> p u t v", v=4),
                    ACT.Ln,
                )

        def subtract(c):
            log_odds[c] = keep.tile([P, CHUNK, PACK], F32, name=f"log_odds{c}")
            nc.vector.tensor_tensor(log_odds[c][:], ln_num[c][:], ln_den[c][:], ALU.subtract)

        def apply_gain(c):
            z_bf[c] = keep.tile([P, CHUNK, PACK], BF16, name=f"z_bf{c}", tag=f"z_bf{c}", align_bytes=64)
            nc.vector.tensor_tensor(
                z_bf[c][:], log_odds[c][:], gain[:].unsqueeze(1).to_broadcast([P, CHUNK, PACK]), ALU.mult
            )

        def project(c):
            cols = slice(CHUNK * c, CHUNK * (c + 1))
            nc.vector.quantize_mx(
                z_codes[:, cols].bitcast(FP8X4), z_scales[:, cols], z_bf[c][:].rearrange("p u t -> p (u t)")
            )
            if c == last_chunk:
                h0_end = psum.tile([P, CHUNK], F32, name="h0_end", tag="y0")
                product(h0_end[:], w2_codes, w2_scales, 0, z_codes, z_scales, cols)
                nc.scalar.copy(window[0][:, cols], h0_end[:])
            else:
                product(h_bank[0][:, cols], w2_codes, w2_scales, 0, z_codes, z_scales, cols)
            if c == last_chunk - 1:
                nc.scalar.copy(window[0][:, : cols.stop], h_bank[0][:, : cols.stop])

        for c in range(chunks // 2):
            logarithms(c)
        subtract(0)
        add_num(LAST, HALF, S)
        for c in range(chunks // 2, chunks):
            logarithms(c)
        for c in range(chunks):
            apply_gain(c)
            if c < last_chunk:
                subtract(c + 1)
            project(c)

        rest_codes, rest_scales = mx_tiles("w2_rest", LAST * P, f"z_bf{last_chunk}")
        for lo, hi in ((0, P), (P, LAST * P)):
            nc.vector.quantize_mx(
                rest_codes[:, lo:hi].bitcast(FP8X4), rest_scales[:, lo:hi], w2_bf[:, PACK * (P + lo) : PACK * (P + hi)]
            )
        for t in range(1, PACK):
            product(h_bank[t][:], rest_codes, rest_scales, t - 1, z_codes, z_scales, slice(0, S))

        out_rows = out.rearrange("(b t r) j -> t b r j", t=PACK, r=BLOCK_ROWS)
        h_n4 = {}

        def gather_n4(t):
            if t > 0:
                nc.scalar.copy(window[t][:, :S], h_bank[t][:])
            h_n4[t] = keep.tile([P, S], F32, name=f"h_n4_{t}")
            nc.vector.tensor_copy(h_n4[t][:], window[t][:].indirect(n4_list[:]))

        gather_n4(0)
        for t in range(PACK):
            if t < LAST:
                gather_n4(t + 1)
            result = keep.tile([P, S], F32, name=f"result{t}")
            bounds = (0, HALF, HALF + CHUNK, S) if t == LAST else (0, S)
            for lo, hi in zip(bounds, bounds[1:]):
                nc.vector.tensor_tensor(
                    result[:, lo:hi], window[t][:].indirect(entries(n5_list, lo, hi)), h_n4[t][:, lo:hi], ALU.mult
                )
                nc.sync.dma_start(out_rows[t][:, :, lo:hi], result[:, lo:hi])
